import numpy as np, ml_dtypes
CORES = [5,13,29,37,53,69,77,101,133,141,157,165,181,197,205,229]
N = 16
import mx_ref
NC, WB = 256, 1
D = 2 * WB + 1
BF = ml_dtypes.bfloat16
def setup_inputs(rng):
    def f(*shape):
        return mx_ref.flush((rng.standard_normal(shape, dtype=np.float32) * np.exp2(rng.integers(-2, 3, shape[:-1] + (1,)))).astype(BF))
    return {"w": f(N, 128, 512), "x": f(N, 128, 4 * NC)}
def reference(w, x):
    QX = [mx_ref.quantize(x[j]) for j in range(N)]
    y = np.zeros((N, 128, D * NC), np.float32)
    for r in range(N):
        qw = mx_ref.quantize(w[r])
        for i in range(D):
            y[r][:, NC * i:NC * i + NC] = mx_ref.matmul(qw, QX[(r + i - WB) % N])
    return {"y": y}

@@ -1,0 +1,239 @@
+from concourse.bass import DstId, RemoteDMATransfer
+from concourse.mybir import dt, ActivationFunctionType
+
+WORLD = 256
+NC = 256
+K_ON = 8
+K_OFF = 8
+QH = 1
+FWD = [("s", 0, NC, 0), ("c", 0, NC, 0)]
+DIR = [("s", 0, NC, 0), ("c", 0, NC, 0)]
+MAXP, MAXG = 4, 2
+
+SCRATCH = {
+    "xb": ("sbuf", [128, 4 * NC], "bfloat16"),
+    "wb": ("sbuf", [128, 512], "bfloat16"),
+    "qx": ("sbuf", [128, NC], "float8_e4m3fn_x4"),
+    "sx": ("sbuf", [128, NC], "uint8"),
+    "qw": ("sbuf", [128, 128], "float8_e4m3fn_x4"),
+    "sw": ("sbuf", [128, 128], "uint8"),
+    "ql": ("sbuf", [128, NC], "float8_e4m3fn_x4"),
+    "sl": ("sbuf", [128, NC], "uint8"),
+    "qr": ("sbuf", [128, NC], "float8_e4m3fn_x4"),
+    "sr": ("sbuf", [128, NC], "uint8"),
+    "ps": ("psum", [128, 512 * 3 * MAXG], "float32"),
+    "yb": ("sbuf", [128, 3 * NC], "float32"),
+}
+SEMAPHORES = (["ldw", "qwd", "sent"] + ["ldx%d" % h for h in range(2)] + ["qxd%d" % h for h in range(2)]
+              + ["rel%d" % p for p in range(MAXP)] + ["a%s%d" % (s, j) for s in "LR" for j in range(MAXG)]
+              + ["%s%d%d" % (n, b, j) for n in ("mm", "cp", "st") for b in range(3) for j in range(MAXG)])
+
+_CACHE = {}
+
+
+def _bits(mask):
+    return [e for e in range(mask.bit_length()) if (mask >> e) & 1]
+
+
+def _masks(allowed, want, n):
+    b = _bits(allowed)
+    k = min(want, len(b) // n)
+    step = len(b) // k
+    return k, [sum(1 << b[i + j * step] for j in range(k)) for i in range(n)]
+
+
+def _plan(T, topo):
+    if "p" in _CACHE:
+        return _CACHE["p"]
+    cores = list(T.cores)
+    n = len(cores)
+
+    def place(c):
+        return (topo.host(c), topo.chip(c))
+
+    def links(src, dst):
+        d, here, ls = topo.die(src), src, []
+        if not topo.same_plane(src, dst):
+            ls.append(("mate", place(src), d))
+            here = [c for c in range(WORLD) if topo.mates(src, c)][0]
+        if place(here) != place(dst):
+            ls += [("out", place(here), d), ("in", place(dst), d)]
+        return ls
+
+    flows = []
+    for r in range(n):
+        for side, step in (("L", 1), ("R", -1)):
+            s, d = cores[r], cores[(r + step) % n]
+            ways = []
+            if topo.may_write(s, d):
+                ways.append((None, links(s, d), 0))
+            for die in (topo.die(s), 1 - topo.die(s)):
+                hs = [c for c in range(WORLD) if place(c) == place(s) and c not in cores
+                      and topo.die(c) == die and topo.may_write(c, d)]
+                if hs:
+                    ways.append((hs, links(hs[0], d), 10 + (die != topo.die(s))))
+            flows.append({"src": s, "dst": d, "side": side, "ways": ways, "way": 0})
+
+    def price():
+        load, p = {}, 0
+        for f in flows:
+            w = f["ways"][f["way"]]
+            p += w[2]
+            for l in w[1]:
+                load[l] = load.get(l, 0) + 1
+        return p + sum(1000 * (v - 1) for v in load.values())
+
+    while True:
+        best, move = price(), None
+        for f in flows:
+            keep = f["way"]
+            for i in range(len(f["ways"])):
+                f["way"] = i
+                p = price()
+                if p < best:
+                    best, move = p, (f, i)
+            f["way"] = keep
+        if move is None:
+            break
+        move[0]["way"] = move[1]
+
+    used = set()
+    for f in sorted(flows, key=lambda f: len(f["ways"][f["way"]][0] or ())):
+        hs, ls, p = f["ways"][f["way"]]
+        f["via"] = None if hs is None else [h for h in hs if h not in used][0]
+        used.add(f["via"])
+        f["late"] = (p, len(ls))
+        f["pieces"] = DIR if hs is None else FWD
+
+    plan = {"out": {}, "in": {}, "fwd": {}}
+    for f in flows:
+        plan["out"].setdefault(f["src"], []).append(f)
+        plan["in"].setdefault(f["dst"], {})[f["side"]] = f
+        if f["via"] is not None:
+            plan["fwd"][f["via"]] = f
+    for c, fs in plan["out"].items():
+        for group, want in (([f for f in fs if f["via"] is not None], K_ON), ([f for f in fs if f["via"] is None], K_OFF)):
+            if group:
+                allowed = topo.mask(c, group[0]["via"] if group[0]["via"] is not None else group[0]["dst"])
+                for f in group[1:]:
+                    allowed &= topo.mask(c, f["via"] if f["via"] is not None else f["dst"])
+                k, ms = _masks(allowed, want, len(group))
+                for f, m in zip(group, ms):
+                    f["k1"], f["m1"] = k, m
+    for f in flows:
+        if f["via"] is not None:
+            k, ms = _masks(topo.mask(f["via"], f["dst"]), K_OFF, 1)
+            f["k2"], f["m2"] = k, ms[0]
+        f["klast"] = f["k2"] if f["via"] is not None else f["k1"]
+    _CACHE["p"] = plan
+    return plan
+
+
+def _emit(g, T, topo, core, items):
+    if len(items) == 1:
+        d, m, out, in_, sem = items[0]
+        rid, pid = topo.addr(d, core)
+        g.remote_dma(out_ap=out, in_ap=in_, remote_sem=sem, local_sem=T.sem.sent, pid=pid, routing_id=rid,
+                     dma_engine_mask=m)
+        return
+    trs = []
+    for d, m, out, in_, sem in items:
+        rid, pid = topo.addr(d, core)
+        trs.append(RemoteDMATransfer(dst_ids=[DstId(rid=rid, pnc=pid)], dma_engine_mask=m, remote_sem=sem,
+                                     src=in_, dst=out))
+    g.remote_dma_fused(trs, local_sem=T.sem.sent)
+
+
+def _view(q, s, piece):
+    kind, a, b, _ = piece
+    return s[:, a:b] if kind == "s" else q[:, a:b].bitcast(dt.uint8)
+
+
+def _landing(T, side):
+    return (T.ql, T.sl) if side == "L" else (T.qr, T.sr)
+
+
+def rank_program(g, core, T, topo):
+    plan = _plan(T, topo)
+    sem = T.sem
+
+    if T.rank_of(core) is None:
+        f = plan["fwd"].get(core)
+        if f is None:
+            return
+        q, s = _landing(T, f["side"])
+        for i, pc in enumerate(f["pieces"]):
+            g.wait_ge(sem["rel%d" % i], f["k1"])
+            _emit(g, T, topo, core, [(f["dst"], f["m2"], _view(q, s, pc), _view(T.qx, T.sx, pc),
+                                      sem["a%s%d" % (f["side"], pc[3])])])
+        g.wait_ge(sem.sent, len(f["pieces"]) * f["k2"])
+        return
+
+    wq = NC // QH
+    for h in range(QH):
+        (g.sync if h == 0 else g.scalar).dma_start(T.xb[:, 4 * wq * h:4 * wq * (h + 1)],
+                                                   T.x[:, 4 * wq * h:4 * wq * (h + 1)]).then_inc(sem["ldx%d" % h], 16)
+    g.sync.dma_start(T.wb[:], T.w[:]).then_inc(sem.ldw, 16)
+    for h in range(QH):
+        g.vector.wait_ge(sem["ldx%d" % h], 16)
+        g.vector.quantize_mx(T.qx[:, wq * h:wq * (h + 1)], T.sx[:, wq * h:wq * (h + 1)],
+                             T.xb[:, 4 * wq * h:4 * wq * (h + 1)]).then_inc(sem["qxd%d" % h], 1)
+    g.vector.wait_ge(sem.ldw, 16)
+    g.vector.quantize_mx(T.qw[:], T.sw[:], T.wb[:]).then_inc(sem.qwd, 1)
+
+    handed = [f for f in plan["out"][core] if f["via"] is not None]
+    straight = [f for f in plan["out"][core] if f["via"] is None]
+    packed, left = 0, 0
+    for fs in (handed, straight):
+        if not fs:
+            continue
+        for i, pc in enumerate(fs[0]["pieces"]):
+            while packed * wq < pc[2]:
+                g.wait_ge(sem["qxd%d" % packed], 1)
+                packed += 1
+            items = []
+            for f in fs:
+                if f["via"] is not None:
+                    items.append((f["via"], f["m1"], _view(T.qx, T.sx, pc), _view(T.qx, T.sx, pc), sem["rel%d" % i]))
+                else:
+                    q, s = _landing(T, f["side"])
+                    items.append((f["dst"], f["m1"], _view(q, s, pc), _view(T.qx, T.sx, pc),
+                                  sem["a%s%d" % (f["side"], pc[3])]))
+                left += f["k1"]
+            _emit(g, T, topo, core, items)
+    g.wait_ge(sem.sent, left)
+
+    inc = plan["in"][core]
+    jobs = [(1, 0, T.qx, T.sx, 0, NC, None, 0)]
+    for side in sorted(("L", "R"), key=lambda s: inc[s]["late"]):
+        f = inc[side]
+        q, s = _landing(T, side)
+        for j in sorted(set(pc[3] for pc in f["pieces"])):
+            mine = [pc for pc in f["pieces"] if pc[3] == j]
+            a = min(pc[1] for pc in mine if pc[0] == "c")
+            b = max(pc[2] for pc in mine if pc[0] == "c")
+            jobs.append((0 if side == "L" else 2, j, q, s, a, b, sem["a%s%d" % (side, j)], len(mine) * f["klast"]))
+    for h in range(QH):
+        g.tensor.wait_ge(sem["qxd%d" % h], 1)
+    g.tensor.wait_ge(sem.qwd, 1)
+    ends = []
+    for pos, (blk, j, q, s, a, b, arr, cnt) in enumerate(jobs):
+        mm, cp, st = sem["mm%d%d" % (blk, j)], sem["cp%d%d" % (blk, j)], sem["st%d%d" % (blk, j)]
+        bank = T.ps[:, 512 * (MAXG * blk + j):512 * (MAXG * blk + j) + (b - a)]
+        cols = slice(NC * blk + a, NC * blk + b)
+        if arr is not None:
+            g.tensor.wait_ge(arr, cnt)
+        g.tensor.matmul_mx(bank, T.qw[:], T.sw[:], q[:, a:b], s[:, a:b], True, True).then_inc(mm, 1)
+        if pos % 2 == 1:
+            g.vector.wait_ge(mm, 1)
+            g.vector.tensor_copy(T.yb[:, cols], bank).then_inc(cp, 1)
+            dq = g.sync
+        else:
+            g.scalar.wait_ge(mm, 1)
+            g.scalar.activation(T.yb[:, cols], bank, ActivationFunctionType.Copy).then_inc(cp, 1)
+            dq = g.scalar
+        dq.wait_ge(cp, 1)
+        dq.dma_start(T.y[:, cols], T.yb[:, cols]).then_inc(st, 16)
+        ends.append((dq, st))
+    for dq, st in ends:
+        dq.wait_ge(st, 16)

@@ -5,8 +5,8 @@ WORLD = 256
 NC = 256
 K_ON = 8
 K_OFF = 8
-QH = 1
-FWD = [("s", 0, NC, 0), ("c", 0, NC, 0)]
+QH = 2
+FWD = [("c", 0, NC // 2, 0), ("s", 0, NC, 0), ("c", NC // 2, NC, 1)]
 DIR = [("s", 0, NC, 0), ("c", 0, NC, 0)]
 MAXP, MAXG = 4, 2
 

from concourse.bass import DstId, RemoteDMATransfer
from concourse.mybir import dt, ActivationFunctionType

WORLD = 256
NC = 256
K_ON = 8
K_OFF = 8
QH = 2
FWD = [("c", 0, NC // 2, 0), ("s", 0, NC, 0), ("c", NC // 2, NC, 1)]
DIR = [("s", 0, NC, 0), ("c", 0, NC, 0)]
MAXP, MAXG = 4, 2

SCRATCH = {
    "xb": ("sbuf", [128, 4 * NC], "bfloat16"),
    "wb": ("sbuf", [128, 512], "bfloat16"),
    "qx": ("sbuf", [128, NC], "float8_e4m3fn_x4"),
    "sx": ("sbuf", [128, NC], "uint8"),
    "qw": ("sbuf", [128, 128], "float8_e4m3fn_x4"),
    "sw": ("sbuf", [128, 128], "uint8"),
    "ql": ("sbuf", [128, NC], "float8_e4m3fn_x4"),
    "sl": ("sbuf", [128, NC], "uint8"),
    "qr": ("sbuf", [128, NC], "float8_e4m3fn_x4"),
    "sr": ("sbuf", [128, NC], "uint8"),
    "ps": ("psum", [128, 512 * 3 * MAXG], "float32"),
    "yb": ("sbuf", [128, 3 * NC], "float32"),
}
SEMAPHORES = (["ldw", "qwd", "sent"] + ["ldx%d" % h for h in range(2)] + ["qxd%d" % h for h in range(2)]
              + ["rel%d" % p for p in range(MAXP)] + ["a%s%d" % (s, j) for s in "LR" for j in range(MAXG)]
              + ["%s%d%d" % (n, b, j) for n in ("mm", "cp", "st") for b in range(3) for j in range(MAXG)])

_CACHE = {}


def _bits(mask):
    return [e for e in range(mask.bit_length()) if (mask >> e) & 1]


def _masks(allowed, want, n):
    b = _bits(allowed)
    k = min(want, len(b) // n)
    step = len(b) // k
    return k, [sum(1 << b[i + j * step] for j in range(k)) for i in range(n)]


def _plan(T, topo):
    if "p" in _CACHE:
        return _CACHE["p"]
    cores = list(T.cores)
    n = len(cores)

    def place(c):
        return (topo.host(c), topo.chip(c))

    def links(src, dst):
        d, here, ls = topo.die(src), src, []
        if not topo.same_plane(src, dst):
            ls.append(("mate", place(src), d))
            here = [c for c in range(WORLD) if topo.mates(src, c)][0]
        if place(here) != place(dst):
            ls += [("out", place(here), d), ("in", place(dst), d)]
        return ls

    flows = []
    for r in range(n):
        for side, step in (("L", 1), ("R", -1)):
            s, d = cores[r], cores[(r + step) % n]
            ways = []
            if topo.may_write(s, d):
                ways.append((None, links(s, d), 0))
            for die in (topo.die(s), 1 - topo.die(s)):
                hs = [c for c in range(WORLD) if place(c) == place(s) and c not in cores
                      and topo.die(c) == die and topo.may_write(c, d)]
                if hs:
                    ways.append((hs, links(hs[0], d), 10 + (die != topo.die(s))))
            flows.append({"src": s, "dst": d, "side": side, "ways": ways, "way": 0})

    def price():
        load, p = {}, 0
        for f in flows:
            w = f["ways"][f["way"]]
            p += w[2]
            for l in w[1]:
                load[l] = load.get(l, 0) + 1
        return p + sum(1000 * (v - 1) for v in load.values())

    while True:
        best, move = price(), None
        for f in flows:
            keep = f["way"]
            for i in range(len(f["ways"])):
                f["way"] = i
                p = price()
                if p < best:
                    best, move = p, (f, i)
            f["way"] = keep
        if move is None:
            break
        move[0]["way"] = move[1]

    used = set()
    for f in sorted(flows, key=lambda f: len(f["ways"][f["way"]][0] or ())):
        hs, ls, p = f["ways"][f["way"]]
        f["via"] = None if hs is None else [h for h in hs if h not in used][0]
        used.add(f["via"])
        f["late"] = (p, len(ls))
        f["pieces"] = DIR if hs is None else FWD

    plan = {"out": {}, "in": {}, "fwd": {}}
    for f in flows:
        plan["out"].setdefault(f["src"], []).append(f)
        plan["in"].setdefault(f["dst"], {})[f["side"]] = f
        if f["via"] is not None:
            plan["fwd"][f["via"]] = f
    for c, fs in plan["out"].items():
        for group, want in (([f for f in fs if f["via"] is not None], K_ON), ([f for f in fs if f["via"] is None], K_OFF)):
            if group:
                allowed = topo.mask(c, group[0]["via"] if group[0]["via"] is not None else group[0]["dst"])
                for f in group[1:]:
                    allowed &= topo.mask(c, f["via"] if f["via"] is not None else f["dst"])
                k, ms = _masks(allowed, want, len(group))
                for f, m in zip(group, ms):
                    f["k1"], f["m1"] = k, m
    for f in flows:
        if f["via"] is not None:
            k, ms = _masks(topo.mask(f["via"], f["dst"]), K_OFF, 1)
            f["k2"], f["m2"] = k, ms[0]
        f["klast"] = f["k2"] if f["via"] is not None else f["k1"]
    _CACHE["p"] = plan
    return plan


def _emit(g, T, topo, core, items):
    if len(items) == 1:
        d, m, out, in_, sem = items[0]
        rid, pid = topo.addr(d, core)
        g.remote_dma(out_ap=out, in_ap=in_, remote_sem=sem, local_sem=T.sem.sent, pid=pid, routing_id=rid,
                     dma_engine_mask=m)
        return
    trs = []
    for d, m, out, in_, sem in items:
        rid, pid = topo.addr(d, core)
        trs.append(RemoteDMATransfer(dst_ids=[DstId(rid=rid, pnc=pid)], dma_engine_mask=m, remote_sem=sem,
                                     src=in_, dst=out))
    g.remote_dma_fused(trs, local_sem=T.sem.sent)


def _view(q, s, piece):
    kind, a, b, _ = piece
    return s[:, a:b] if kind == "s" else q[:, a:b].bitcast(dt.uint8)


def _landing(T, side):
    return (T.ql, T.sl) if side == "L" else (T.qr, T.sr)


def rank_program(g, core, T, topo):
    plan = _plan(T, topo)
    sem = T.sem

    if T.rank_of(core) is None:
        f = plan["fwd"].get(core)
        if f is None:
            return
        q, s = _landing(T, f["side"])
        for i, pc in enumerate(f["pieces"]):
            g.wait_ge(sem["rel%d" % i], f["k1"])
            _emit(g, T, topo, core, [(f["dst"], f["m2"], _view(q, s, pc), _view(T.qx, T.sx, pc),
                                      sem["a%s%d" % (f["side"], pc[3])])])
        g.wait_ge(sem.sent, len(f["pieces"]) * f["k2"])
        return

    wq = NC // QH
    for h in range(QH):
        (g.sync if h == 0 else g.scalar).dma_start(T.xb[:, 4 * wq * h:4 * wq * (h + 1)],
                                                   T.x[:, 4 * wq * h:4 * wq * (h + 1)]).then_inc(sem["ldx%d" % h], 16)
    g.sync.dma_start(T.wb[:], T.w[:]).then_inc(sem.ldw, 16)
    for h in range(QH):
        g.vector.wait_ge(sem["ldx%d" % h], 16)
        g.vector.quantize_mx(T.qx[:, wq * h:wq * (h + 1)], T.sx[:, wq * h:wq * (h + 1)],
                             T.xb[:, 4 * wq * h:4 * wq * (h + 1)]).then_inc(sem["qxd%d" % h], 1)
    g.vector.wait_ge(sem.ldw, 16)
    g.vector.quantize_mx(T.qw[:], T.sw[:], T.wb[:]).then_inc(sem.qwd, 1)

    handed = [f for f in plan["out"][core] if f["via"] is not None]
    straight = [f for f in plan["out"][core] if f["via"] is None]
    packed, left = 0, 0
    for fs in (handed, straight):
        if not fs:
            continue
        for i, pc in enumerate(fs[0]["pieces"]):
            while packed * wq < pc[2]:
                g.wait_ge(sem["qxd%d" % packed], 1)
                packed += 1
            items = []
            for f in fs:
                if f["via"] is not None:
                    items.append((f["via"], f["m1"], _view(T.qx, T.sx, pc), _view(T.qx, T.sx, pc), sem["rel%d" % i]))
                else:
                    q, s = _landing(T, f["side"])
                    items.append((f["dst"], f["m1"], _view(q, s, pc), _view(T.qx, T.sx, pc),
                                  sem["a%s%d" % (f["side"], pc[3])]))
                left += f["k1"]
            _emit(g, T, topo, core, items)
    g.wait_ge(sem.sent, left)

    inc = plan["in"][core]
    jobs = [(1, 0, T.qx, T.sx, 0, NC, None, 0)]
    for side in sorted(("L", "R"), key=lambda s: inc[s]["late"]):
        f = inc[side]
        q, s = _landing(T, side)
        for j in sorted(set(pc[3] for pc in f["pieces"])):
            mine = [pc for pc in f["pieces"] if pc[3] == j]
            a = min(pc[1] for pc in mine if pc[0] == "c")
            b = max(pc[2] for pc in mine if pc[0] == "c")
            jobs.append((0 if side == "L" else 2, j, q, s, a, b, sem["a%s%d" % (side, j)], len(mine) * f["klast"]))
    for h in range(QH):
        g.tensor.wait_ge(sem["qxd%d" % h], 1)
    g.tensor.wait_ge(sem.qwd, 1)
    ends = []
    for pos, (blk, j, q, s, a, b, arr, cnt) in enumerate(jobs):
        mm, cp, st = sem["mm%d%d" % (blk, j)], sem["cp%d%d" % (blk, j)], sem["st%d%d" % (blk, j)]
        bank = T.ps[:, 512 * (MAXG * blk + j):512 * (MAXG * blk + j) + (b - a)]
        cols = slice(NC * blk + a, NC * blk + b)
        if arr is not None:
            g.tensor.wait_ge(arr, cnt)
        g.tensor.matmul_mx(bank, T.qw[:], T.sw[:], q[:, a:b], s[:, a:b], True, True).then_inc(mm, 1)
        if pos % 2 == 1:
            g.vector.wait_ge(mm, 1)
            g.vector.tensor_copy(T.yb[:, cols], bank).then_inc(cp, 1)
            dq = g.sync
        else:
            g.scalar.wait_ge(mm, 1)
            g.scalar.activation(T.yb[:, cols], bank, ActivationFunctionType.Copy).then_inc(cp, 1)
            dq = g.scalar
        dq.wait_ge(cp, 1)
        dq.dma_start(T.y[:, cols], T.yb[:, cols]).then_inc(st, 16)
        ends.append((dq, st))
    for dq, st in ends:
        dq.wait_ge(st, 16)
